import numpy as np, ml_dtypes
CORES = [24,26,29,31,48,50,53,55]
N = 8
TOK, K, FT = 32, 2, 4
ROUTE = [[[4,5],[5,6],[2,3],[2,5],[1,6],[2,4],[4,6],[5,7],[1,5],[4,7],[3,6],[3,7],[1,6],[3,5],[4,7],[4,5],[2,3],[3,6],[0,3],[3,7],[0,5],[2,7],[4,7],[4,5],[1,4],[3,7],[0,3],[3,5],[3,5],[4,6],[3,5],[2,3]],[[2,6],[2,4],[5,7],[0,5],[2,6],[3,4],[2,6],[2,6],[0,2],[2,6],[0,1],[1,2],[1,6],[1,2],[0,4],[1,2],[1,2],[4,5],[0,5],[0,4],[6,7],[1,5],[0,4],[2,5],[2,4],[6,7],[3,4],[6,7],[5,6],[1,4],[1,7],[4,7]],[[0,3],[0,4],[1,3],[1,7],[3,4],[0,5],[2,4],[1,5],[1,3],[4,5],[1,2],[0,4],[1,2],[0,1],[2,6],[4,7],[2,6],[2,6],[1,4],[1,3],[2,3],[0,1],[2,7],[1,3],[1,4],[0,4],[1,2],[0,1],[2,6],[2,3],[1,4],[1,5]],[[5,7],[1,6],[3,7],[1,2],[0,5],[1,4],[0,3],[2,4],[3,7],[5,6],[2,7],[0,7],[1,3],[4,5],[2,6],[0,7],[5,7],[0,1],[0,4],[2,7],[4,5],[3,7],[4,7],[0,2],[0,3],[0,5],[2,6],[2,5],[0,3],[0,7],[1,6],[3,7]],[[2,7],[2,6],[1,3],[5,7],[2,6],[0,7],[0,2],[6,7],[2,5],[6,7],[5,6],[0,4],[0,4],[1,4],[2,3],[2,6],[1,3],[0,6],[0,6],[1,2],[6,7],[1,6],[1,3],[1,2],[0,6],[3,6],[1,4],[1,6],[0,4],[0,4],[0,4],[0,5]],[[1,4],[0,6],[4,7],[0,6],[4,5],[1,4],[0,1],[0,1],[0,4],[0,2],[6,7],[1,5],[0,6],[3,6],[0,7],[3,5],[2,5],[4,7],[3,7],[1,5],[1,5],[4,7],[1,2],[0,5],[0,1],[0,7],[2,4],[2,5],[2,5],[0,1],[0,5],[2,6]],[[1,3],[2,7],[0,3],[2,6],[4,7],[5,7],[4,5],[6,7],[0,6],[0,4],[0,4],[3,5],[0,7],[0,7],[4,6],[4,6],[5,7],[2,6],[5,7],[4,5],[0,7],[3,6],[4,7],[0,7],[1,3],[3,6],[1,7],[2,6],[5,6],[4,7],[4,5],[2,5]],[[2,4],[1,4],[0,5],[3,4],[3,6],[3,7],[5,6],[1,3],[0,5],[0,4],[0,4],[2,3],[6,7],[4,5],[4,5],[4,7],[1,6],[1,2],[2,4],[0,7],[6,7],[1,7],[2,7],[4,6],[0,4],[2,7],[4,5],[3,4],[2,5],[0,5],[3,4],[2,3]]]
def setup_inputs(rng):
    return {"x": rng.standard_normal((N, 128, TOK), dtype=np.float32).astype(ml_dtypes.bfloat16), "gate": (0.5 * rng.integers(1, 4, size=(N, K, TOK)) * (2 * rng.integers(0, 2, size=(N, K, TOK)) - 1)).astype(np.float32).astype(ml_dtypes.bfloat16), "w1": (rng.standard_normal((N, 128, FT * 128), dtype=np.float32) / 8).astype(ml_dtypes.bfloat16), "w2": (rng.standard_normal((N, 128, FT * 128), dtype=np.float32) / 8).astype(ml_dtypes.bfloat16)}
def setup_inputs_big(rng):
    d = setup_inputs(rng)
    for k in ("x", "gate", "w1", "w2"): d[k] = (d[k].astype(np.float32) * 1024.0).astype(d[k].dtype)
    return d
def setup_inputs_small(rng):
    d = setup_inputs(rng)
    for k in ("x", "gate", "w1", "w2"): d[k] = (d[k].astype(np.float32) * (1 / 1024.0)).astype(d[k].dtype)
    return d
def reference(x, gate, w1, w2):
    X, GATE, W1, W2 = x.astype(np.float64), gate.astype(np.float64), w1.astype(np.float64), w2.astype(np.float64)
    y = np.zeros((N, 128, TOK))
    for r in range(N):
        for t in range(TOK):
            for i, e in enumerate(ROUTE[r][t]):
                hid = np.maximum(W1[e].T @ X[r][:, t], 0.0)
                y[r][:, t] += GATE[r][i, t] * sum(W2[e][:, 128 * f:128 * f + 128].T @ hid[128 * f:128 * f + 128] for f in range(FT))
    return {"y": y.astype(ml_dtypes.bfloat16)}

from concourse.bass import DstId, RemoteDMATransfer
from concourse.mybir import AluOpType

BF, F32 = "bfloat16", "float32"
SCRATCH = {
    "XC": ("sbuf", [128, 128], BF),
    "XP": ("sbuf", [128, 64], BF),
    "XQ": ("sbuf", [128, 64], BF),
    "W": ("sbuf", [128, 1024], BF),
    "WR": ("sbuf", [128, 1024], BF),
    "GROW": ("sbuf", [128, 64], BF),
    "ONES": ("sbuf", [128, 128], BF),
    "ZER": ("sbuf", [128, 512], F32),
    "HA": ("sbuf", [128, 512], BF),
    "HPa": ("sbuf", [128, 256], BF), "HPb": ("sbuf", [128, 256], BF),
    "HQa": ("sbuf", [128, 256], BF), "HQb": ("sbuf", [128, 256], BF),
    "RA": ("sbuf", [128, 128], BF),
    "RP": ("sbuf", [128, 128], BF),
    "RQ": ("sbuf", [128, 128], BF),
    "LAND": ("sbuf", [128, 256], BF),
    "PN": ("sbuf", [128, 128], F32), "PF": ("sbuf", [128, 128], F32),
    "S1": ("sbuf", [128, 64], F32), "T1": ("sbuf", [128, 64], F32),
    "ACC": ("sbuf", [128, 32], F32), "T2": ("sbuf", [128, 32], F32),
    "Y": ("sbuf", [128, 32], BF),
    "pHA": ("psum", [128, 512], F32), "pOA": ("psum", [128, 512], F32),
    "pHa": ("psum", [128, 512], F32), "pHb": ("psum", [128, 512], F32),
    "pOa": ("psum", [128, 512], F32), "pOb": ("psum", [128, 512], F32),
    "pG": ("psum", [128, 512], F32),
}
SEMAPHORES = ["x", "g", "w", "c", "z", "gm", "xn", "xp", "rp", "rq", "wr", "la", "lr", "loc",
              "hA", "rA", "oA", "eA", "eL",
              "hPa", "hPb", "rPa", "rPb", "oPa", "oPb", "ePa", "ePb",
              "hQa", "hQb", "rQa", "rQb", "oQa", "oQb", "eQa", "eQb",
              "v1", "v2", "v3", "v4", "v5", "v6", "y", "st"]


def _bits(m):
    return [i for i in range(m.bit_length()) if (m >> i) & 1]


def _mk(engines):
    m = 0
    for e in engines:
        m |= 1 << e
    return m


def _chip_plan(ranks, cores, far_core, topo):
    srv = [r for r in ranks if topo.may_write(cores[r], far_core)]
    rest = [r for r in ranks if r not in srv]
    leaves = []
    for s in srv:
        same = [r for r in rest if r not in leaves and topo.die(cores[r]) == topo.die(cores[s])]
        leaves.append(same[0])
    return srv, leaves


def _ret_engines(sender, srv, xorder, cores, far_core, topo):
    dests = [r for r in xorder if r != sender]
    on = _bits(topo.mask(cores[sender], cores[dests[0]]))
    if sender in srv:
        off = _bits(topo.mask(cores[sender], far_core))
        free = [b for b in on if b not in off]
        h = len(free) // 2
        parts = [free[0:h], free[h:h + h // 2], free[h + h // 2:h + h]]
    else:
        q = len(on) // 4
        parts = [on[0:q], on[q:2 * q], on[2 * q:3 * q]]
    return {d: parts[i] for i, d in enumerate(dests)}


def rank_program(g, core, T, topo):
    rank = T.rank_of(core)
    if rank is None:
        return
    cores = list(T.cores)
    TOK, FT, ROUTE = T.tables["TOK"], T.tables["FT"], T.tables["ROUTE"]
    S = T.sem
    pe, ve = g.tensor, g.vector

    mychip = topo.chip(core)
    near = [r for r in range(len(cores)) if topo.chip(cores[r]) == mychip]
    far = [r for r in range(len(cores)) if topo.chip(cores[r]) != mychip]
    srv, leaves = _chip_plan(near, cores, cores[far[0]], topo)
    fsrv, fleaves = _chip_plan(far, cores, cores[near[0]], topo)
    xorder = leaves + srv
    eorder = [r for k in range(len(srv)) for r in (leaves[k], srv[k])]
    feorder = [r for k in range(len(fsrv)) for r in (fleaves[k], fsrv[k])]
    landpos = {e: i for i, e in enumerate(eorder + feorder)}
    server = rank in srv
    mypos = xorder.index(rank)
    NL = len(leaves) * TOK
    NC = len(xorder) * TOK

    def blk(buf, i, w=TOK):
        return buf[:, i * w:(i + 1) * w]

    def dst_id(r):
        rid, pid, _ = topo.addr(cores[r])
        return DstId(rid=rid, pnc=pid)

    sent = [0]

    def fused(transfers):
        for tr, n in transfers:
            sent[0] += n
        g.remote_dma_fused([tr for tr, n in transfers], local_sem=S.loc)

    def xfer(src, dst, dests, engines, sem):
        return (RemoteDMATransfer(dst_ids=[dst_id(r) for r in dests], dma_engine_mask=_mk(engines), remote_sem=sem,
                                  srcs=[src], dsts=[dst for r in dests]), len(engines))

    on = _bits(topo.mask(core, cores[[r for r in near if r != rank][0]]))
    off = _bits(topo.mask(core, cores[far[0]]))
    hi = [b for b in on if b not in off]
    half = len(off) // 2

    g.sync.dma_start(blk(T.XC, mypos), T.x[:, :]).then_inc(S.x, 16)
    g.scalar.dma_start(T.GROW[0:1, 0:TOK], T.gate[0:1, :]).then_inc(S.g, 16)
    g.scalar.dma_start(T.GROW[0:1, TOK:2 * TOK], T.gate[1:2, :]).then_inc(S.g, 16)
    g.sync.dma_start(T.W[:, 0:512], T.w1[:, :]).then_inc(S.w, 16)
    g.scalar.dma_start(T.W[:, 512:1024], T.w2[:, :]).then_inc(S.w, 16)

    ve.memset(T.ONES[0:1, :], 1.0).then_inc(S.c, 1)
    ve.memset(T.pG[:, 0:256], 0.0).then_inc(S.c, 1)
    ve.memset(T.ZER[:, :], 0.0).then_inc(S.z, 1)

    pe.wait_ge(S.c, 2)
    pe.wait_ge(S.g, 32)
    ngm = 0
    for i in range(len(ROUTE[rank][0])):
        t = 0
        while t < TOK:
            e = ROUTE[rank][t][i]
            n = 1
            while t + n < TOK and ROUTE[rank][t + n][i] == e:
                n += 1
            c0 = landpos[e] * TOK + t
            pe.matmul(T.pG[:, c0:c0 + n], T.ONES[0:1, :], T.GROW[0:1, i * TOK + t:i * TOK + t + n],
                      start=True, stop=True).then_inc(S.gm, 1)
            ngm += 1
            t += n

    n_xn = sum((half if server else 2 * half) for r in leaves if r != rank)
    n_xp = sum(len(hi) for r in srv if r != rank)
    n_la = sum(len(_ret_engines(s, srv, xorder, cores, cores[far[0]], topo)[rank]) for s in near if s != rank)
    n_lr = half * len(fsrv)

    g.wait_ge(S.x, 16)
    if server:
        k = srv.index(rank)
        fused([xfer(blk(T.XC, mypos), blk(T.XP, k), fsrv, off, S.rp),
               xfer(blk(T.XC, mypos), blk(T.XC, mypos), [r for r in xorder if r != rank], hi, S.xp)])
        g.wait_ge(S.xn, n_xn)
        fused([xfer(T.XC[:, 0:NL], T.XQ[:, :], [fsrv[k]], off, S.rq)])
    else:
        fused([xfer(blk(T.XC, mypos), blk(T.XC, mypos), [s], on[j * half:(j + 1) * half], S.xn)
               for j, s in enumerate(srv)])
        fused([xfer(blk(T.XC, mypos), blk(T.XC, mypos), [r for r in leaves if r != rank], on[0:2 * half], S.xn)])
        g.wait_ge(S.w, 32)
        fused([xfer(T.W[:, :], T.WR[:, :], [srv[leaves.index(rank)]], on, S.wr)])
    g.wait_ge(S.eA, 1)
    eng = _ret_engines(rank, srv, xorder, cores, cores[far[0]], topo)
    fused([xfer(blk(T.RA, xorder.index(r)), blk(T.LAND, landpos[rank]), [r], eng[r], S.la)
           for r in xorder if r != rank])
    if server:
        home = T.LAND[:, (len(eorder) + 2 * k) * TOK:(len(eorder) + 2 * k + 2) * TOK]
        for R, ea, eb, dests in ((T.RP, S.ePa, S.ePb, fsrv), (T.RQ, S.eQa, S.eQb, fleaves)):
            g.wait_ge(ea, len(dests))
            g.wait_ge(eb, len(dests))
            fused([xfer(blk(R, j, 2 * TOK), home, [r], off[j * half:(j + 1) * half], S.lr)
                   for j, r in enumerate(dests)])
    g.wait_ge(S.loc, sent[0])

    def layer1(Wt, X, n, pH, sem):
        for f in range(FT):
            pe.matmul(pH[:, f * n:(f + 1) * n], Wt[:, f * 128:(f + 1) * 128], X, start=True, stop=True).then_inc(sem, 1)

    def relu(H, pH, n, sem_in, sem_out):
        ve.wait_ge(sem_in, FT)
        ve.tensor_tensor(H[:, 0:FT * n], pH[:, 0:FT * n], T.ZER[:, 0:FT * n], AluOpType.max).then_inc(sem_out, 1)

    def layer2(Wt, H, n, pO, sem):
        for f in range(FT):
            pe.matmul(pO[:, 0:n], Wt[:, 512 + f * 128:512 + (f + 1) * 128], H[:, f * n:(f + 1) * n],
                      start=(f == 0), stop=(f == FT - 1)).then_inc(sem, 1)

    pe.wait_ge(S.x, 16)
    pe.wait_ge(S.xn, n_xn)
    pe.wait_ge(S.xp, n_xp)
    pe.wait_ge(S.w, 32)
    layer1(T.W, T.XC[:, :], NC, T.pHA, S.hA)
    ve.wait_ge(S.z, 1)
    relu(T.HA, T.pHA, NC, S.hA, S.rA)
    pe.wait_ge(S.rA, 1)
    layer2(T.W, T.HA, NC, T.pOA, S.oA)
    ve.wait_ge(S.oA, FT)
    ve.tensor_copy(T.RA[:, :], T.pOA[:, 0:NC]).then_inc(S.eA, 1)
    ve.tensor_copy(blk(T.LAND, landpos[rank]), blk(T.pOA, mypos)).then_inc(S.eL, 1)

    if server:
        waves = ((T.XP, S.rp, len(off) * len(fsrv), T.HPa, T.HPb, T.RP,
                  S.hPa, S.hPb, S.rPa, S.rPb, S.oPa, S.oPb, S.ePa, S.ePb),
                 (T.XQ, S.rq, len(off), T.HQa, T.HQb, T.RQ,
                  S.hQa, S.hQb, S.rQa, S.rQb, S.oQa, S.oQb, S.eQa, S.eQb))
        prev = None
        for wv, (X, sx, nx, Ha, Hb, R, ha, hb, ra, rb, oa, ob, ea, eb) in enumerate(waves):
            nsrc = NL // TOK
            pe.wait_ge(sx, nx)
            layer1(T.W, X[:, :], NL, T.pHa, ha)
            if wv == 0:
                pe.wait_ge(S.wr, len(on))
            layer1(T.WR, X[:, :], NL, T.pHb, hb)
            relu(Ha, T.pHa, NL, ha, ra)
            relu(Hb, T.pHb, NL, hb, rb)
            pe.wait_ge(ra, 1)
            if prev:
                pe.wait_ge(prev[0], nsrc)
            layer2(T.W, Ha, NL, T.pOa, oa)
            pe.wait_ge(rb, 1)
            if prev:
                pe.wait_ge(prev[1], nsrc)
            layer2(T.WR, Hb, NL, T.pOb, ob)
            ve.wait_ge(oa, FT)
            for j in range(nsrc):
                ve.tensor_copy(blk(R, 2 * j + 1), blk(T.pOa, j)).then_inc(ea, 1)
            ve.wait_ge(ob, FT)
            for j in range(nsrc):
                ve.tensor_copy(blk(R, 2 * j), blk(T.pOb, j)).then_inc(eb, 1)
            prev = (ea, eb)

    def tt(out, a, b, op, sem):
        ve.tensor_tensor(out, a, b, op).then_inc(sem, 1)
        ve.wait_ge(sem, 1)

    ve.wait_ge(S.gm, ngm)
    ve.wait_ge(S.eL, 1)
    ve.wait_ge(S.la, n_la)
    tt(T.PN[:, :], T.LAND[:, 0:128], T.pG[:, 0:128], AluOpType.mult, S.v1)
    tt(T.S1[:, :], T.PN[:, 0:64], T.PN[:, 64:128], AluOpType.add, S.v2)
    tt(T.ACC[:, :], T.S1[:, 0:32], T.S1[:, 32:64], AluOpType.add, S.v3)
    ve.wait_ge(S.lr, n_lr)
    tt(T.PF[:, :], T.LAND[:, 128:256], T.pG[:, 128:256], AluOpType.mult, S.v4)
    tt(T.T1[:, :], T.PF[:, 0:64], T.PF[:, 64:128], AluOpType.add, S.v5)
    tt(T.T2[:, :], T.T1[:, 0:32], T.T1[:, 32:64], AluOpType.add, S.v6)
    ve.tensor_tensor(T.Y[:, :], T.T2[:, :], T.ACC[:, :], AluOpType.add).then_inc(S.y, 1)
    g.sync.wait_ge(S.y, 1)
    g.sync.dma_start(T.y[:, :], T.Y[:, :]).then_inc(S.st, 16)
    g.sync.wait_ge(S.st, 16)
